import numpy as np
import ml_dtypes


def mxq(x, axis, fmt="e4m3"):
    dtype, down = {"e4m3": (ml_dtypes.float8_e4m3fn, 7), "e5m2": (ml_dtypes.float8_e5m2, 14)}[fmt]
    v = np.moveaxis(np.asarray(x, np.float32).astype(ml_dtypes.bfloat16).astype(np.float64), axis, -1)
    blocks = v.reshape(v.shape[:-1] + (-1, 32))
    amax = np.abs(blocks).max(-1, keepdims=True)
    byte = np.maximum(np.where(amax > 0, np.frexp(amax)[1] - 1 + 127, 0) - down, 1)
    scale = np.exp2(byte - 127.0)
    codes = (blocks / scale).astype(np.float32).astype(dtype).astype(np.float64)
    return np.moveaxis((codes * scale).reshape(v.shape), -1, axis)


WIDE = False


def mx_kscale(k):
    if not WIDE:
        return np.ones(k)
    levels = np.array([10, -10, 5, -5, 0])
    if k % 512:
        return np.exp2(np.random.permutation(np.resize(levels, k // 32))).repeat(32)
    a = np.empty((k // 512, 16))
    for p in range(k // 512):
        a[p, :8] = np.random.permutation(np.resize(levels, 8))
        for g in range(8):
            far = levels[np.abs(levels - a[p, g]) >= 10]
            a[p, g + 8] = far[np.random.randint(len(far))]
    return np.exp2(a.ravel()).repeat(32)


def f64(x):
    return np.asarray(x).astype(np.float64)


def striped(idx):
    return np.tile(idx.reshape(-1, 16).T, (8, 1)).astype(np.uint16)


def unstriped(offs):
    return offs[:16].T.reshape(-1).astype(np.int64)


E2M1 = np.array([0.0, 0.5, 1.0, 1.5, 2.0, 3.0, 4.0, 6.0, -0.0, -0.5, -1.0, -1.5, -2.0, -3.0, -4.0, -6.0])


def pack_weight(w, fmt):
    k, n = w.shape
    w = f64(np.asarray(w, np.float32).astype(ml_dtypes.bfloat16)).reshape(k // 32, 32, n)
    amax = np.abs(w).max(1)
    if fmt == "e4m3":
        byte = np.frexp(amax)[1] - 1 + 127 - 7
    else:
        mant, ex = np.frexp(amax / 6.0)
        byte = np.where(mant > 0.5, ex, ex - 1) + 127
    byte = np.clip(np.where(amax > 0, byte, 1), 1, 254)
    scaled = (w * np.exp2(127.0 - byte)[:, None, :]).reshape(k, n).astype(np.float32)
    by_word = np.ascontiguousarray(scaled.reshape(k // 512, 128, 4, n).transpose(0, 1, 3, 2))
    if fmt == "e4m3":
        words = by_word.astype(ml_dtypes.float8_e4m3fn).view(np.uint8)
    else:
        c = by_word.astype(ml_dtypes.float4_e2m1fn).view(np.uint8) & 0xF
        words = (c[..., 0::2] | (c[..., 1::2] << 4)).reshape(k // 512, 128, 2 * n)
    return np.ascontiguousarray(words), np.ascontiguousarray(byte.astype(np.uint8).reshape(k // 512, 16, n))


def unpack_weight(words, scales, fmt):
    g, _, n = scales.shape
    words = np.ascontiguousarray(words).reshape(g, 128, n, -1)
    if fmt == "e4m3":
        vals = words.view(ml_dtypes.float8_e4m3fn).astype(np.float64)
    else:
        nib = np.empty((g, 128, n, 4), np.uint8)
        nib[..., 0::2] = words & 0xF
        nib[..., 1::2] = words >> 4
        vals = E2M1[nib]
    vals = vals * np.repeat(np.exp2(scales.astype(np.float64) - 127.0), 8, axis=1)[..., None]
    return vals.transpose(0, 1, 3, 2).reshape(g * 512, n)


def relu(v):
    return np.maximum(v, 0.0)


K, T, E, C, N = 1024, 1024, 8, 128, 384


def by_expert(wq, xq):
    return np.concatenate([wq[e].T @ xq[:, e * C:(e + 1) * C] for e in range(E)], axis=1)


def setup_inputs():
    n = np.random.standard_normal
    s = mx_kscale(K)[:, None]
    w = [pack_weight(m, "e2m1") for m in n((E + 1, K, N)) / np.sqrt(K) / s[None]]
    return {
        "xT": (n((K, T)) * s).astype(np.float32),
        "w_words": np.stack([m[0] for m in w]),
        "w_scales": np.stack([m[1] for m in w]),
        "b": (0.3 * n((N, E + 1))).astype(np.float32),
        "gate": np.tile(np.random.uniform(0.2, 1.0, E * C), (N, 1)).astype(np.float32),
        "offs": striped(np.random.permutation(T)[:E * C]),
    }


def reference(xT, w_words, w_scales, b, gate, offs):
    idx = unstriped(offs)
    w = np.stack([unpack_weight(w_words[e], w_scales[e], "e2m1") for e in range(E + 1)])
    wq = w
    xs = mxq(f64(xT), 0, "e4m3")
    ys = relu((wq[E].T @ xs) + f64(b)[:, E:])
    xq = mxq(f64(xT)[:, idx], 0, "e4m3")
    y = by_expert(w, xq)
    y = relu(y + np.repeat(f64(b)[:, :E], C, axis=1))
    out = ys
    out[:, idx] += f64(gate) * y
    return out

@@ -1,0 +1,195 @@
+from contextlib import ExitStack
+
+import concourse.mybir as mybir
+
+K, T, E, C, N = 1024, 1024, 8, 128, 384
+
+F32 = mybir.dt.float32
+BF16 = mybir.dt.bfloat16
+I32 = mybir.dt.int32
+U32 = mybir.dt.uint32
+U16 = mybir.dt.uint16
+U8 = mybir.dt.uint8
+FP8X4 = mybir.dt.float8_e4m3fn_x4
+FP4X4 = mybir.dt.float4_e2m1fn_x4
+COPY = mybir.ActivationFunctionType.Copy
+RELU = mybir.ActivationFunctionType.Relu
+MULT = mybir.AluOpType.mult
+ADD = mybir.AluOpType.add
+
+P = 128
+PASSES = K // 512
+H = 512
+NT = N // P
+W_LOADS = ((E, 1), (0, 2), (2, 2), (4, 4))
+
+FLOPS = 2 * K * N * T * 2
+BYTES = K * T * 4 + (E + 1) * K * N // 2 + (E + 1) * (K // 32) * N + N * (E + 1) * 4 + E * C * 4 + E * C * 2 + N * T * 4
+
+
+def tile_moe_shr_lin_relu_kernel(tc, xT, w_words, w_scales, b, gate, offs, out):
+    nc = tc.nc
+    with ExitStack() as ctx:
+        held = ctx.enter_context(tc.tile_pool(name="held", bufs=1))
+        work = ctx.enter_context(tc.tile_pool(name="work", bufs=3))
+        psum = ctx.enter_context(tc.psum_pool(name="psum", bufs=8))
+
+        offsets = held.tile([P, E * C // 16], U16, name="offsets")
+        nc.sync.dma_start(offsets[:], offs)
+
+        bias = held.tile([P, NT, E + 1], F32, name="bias")
+        nc.scalar.dma_start(out=bias[:], in_=b.rearrange("(t p) e -> p t e", p=P))
+
+        raw = [[held.tile([P, 2, T], F32, name=f"raw{a}{u}") for u in range(2)] for a in range(PASSES)]
+        pair = [[held.tile([P, 2 * T], BF16, name=f"pair{a}{u}", align_bytes=64) for u in range(2)] for a in range(PASSES)]
+        for a in range(PASSES):
+            rows = xT[512 * a : 512 * (a + 1), :].rearrange("(p j) w -> p j w", j=4)
+            for u in range(2):
+                for c in range(2):
+                    cols = slice(512 * c, 512 * (c + 1))
+                    nc.sync.dma_start(out=raw[a][u][:, :, cols], in_=rows[:, 2 * u : 2 * u + 2, cols])
+
+        w_sc = held.tile([P, (E + 1) * PASSES * N], U8, name="w_sc", align_bytes=64)
+        nc.vector.memset(w_sc[:].bitcast(I32), 0)
+        scales_in = w_scales.bitcast(I32)
+        for q in range(4):
+            nc.sync.dma_start(
+                out=w_sc[32 * q : 32 * q + 4, :].bitcast(I32).rearrange("q (g n) -> q g n", n=N // 4),
+                in_=scales_in[:, :, 4 * q : 4 * q + 4, :].rearrange("e a q n -> q (e a) n"),
+            )
+        w_tile = [held.tile([P, n, PASSES, 2 * N], U8, name=f"w_tile{i}", align_bytes=64) for i, (e, n) in enumerate(W_LOADS)]
+        gates = [held.tile([P, H], F32, name=f"gates{h}") for h in range(2)]
+        words_in = w_words.bitcast(I32)
+
+        def load_words(i):
+            e, n = W_LOADS[i]
+            nc.sync.dma_start(
+                out=w_tile[i][:].rearrange("p e a n -> p (e a n)").bitcast(I32).rearrange("p (g n) -> p g n", n=N // 2),
+                in_=words_in[e : e + n].rearrange("e a p n -> p (e a) n"),
+            )
+
+        def load_gates(h):
+            nc.sync.dma_start(out=gates[h][:], in_=gate[0:P, H * h : H * (h + 1)])
+
+        load_words(0)
+        load_words(1)
+        load_gates(0)
+        load_words(2)
+        load_words(3)
+        load_gates(1)
+
+        def words_of(e, a, t):
+            for i, (first, n) in enumerate(W_LOADS):
+                if first <= e < first + n:
+                    return w_tile[i][:, e - first, a, 2 * P * t : 2 * P * (t + 1)].bitcast(FP4X4)
+
+        def cast(engine_call, a, u, c0, c1):
+            engine_call(
+                pair[a][u][:, 2 * c0 : 2 * c1].rearrange("p (w j) -> p w j", j=2),
+                raw[a][u][:, :, c0:c1].rearrange("p j w -> p w j"),
+            )
+
+        planes = [[held.tile([P, 2, H], U32, name=f"planes{a}{h}", align_bytes=64) for h in range(2)] for a in range(PASSES)]
+        grouped = [[held.tile([P, 4 * H], BF16, name=f"grouped{a}{h}", align_bytes=64) for h in range(2)] for a in range(PASSES)]
+        codes = [[held.tile([P, H], U32, name=f"codes{a}{h}", align_bytes=64) for h in range(2)] for a in range(PASSES)]
+        x_sc = [[held.tile([P, H], U8, name=f"x_sc{a}{h}", align_bytes=64) for h in range(2)] for a in range(PASSES)]
+
+        def window(a, u, h):
+            return pair[a][u][:].bitcast(U32).indirect(offsets[:, 32 * h : 32 * (h + 1)])
+
+        def gather_plain(a, u, h):
+            nc.vector.tensor_copy(planes[a][h][:, u, :], window(a, u, h))
+
+        def gather_step(a, u, h):
+            nc.vector.tensor_copy(grouped[a][h][:].bitcast(U32).rearrange("p (s u) -> p s u", u=2)[:, :, u], window(a, u, h))
+
+        def weave_scalar(a, h, s0, s1):
+            src = planes[a][h][:].rearrange("p u s -> p (u s)").bitcast(BF16).rearrange("p (u s j) -> p s u j", u=2, j=2)
+            nc.scalar.copy(grouped[a][h][:].rearrange("p (s u j) -> p s u j", u=2, j=2)[:, s0:s1], src[:, s0:s1])
+
+        def weave_gpsimd(a, h, s0, s1):
+            nc.gpsimd.tensor_copy(
+                grouped[a][h][:].bitcast(U32).rearrange("p (s u) -> p s u", u=2)[:, s0:s1],
+                planes[a][h][:, :, s0:s1].rearrange("p u s -> p s u"),
+            )
+
+        def quantise(a, h):
+            nc.vector.quantize_mx(out=codes[a][h][:].bitcast(FP8X4), scales=x_sc[a][h][:], in_=grouped[a][h][:])
+
+        for i in range(4):
+            a, u = divmod(i, 2)
+            cast(nc.scalar.copy, a, u, 0, 256)
+            cast(nc.gpsimd.tensor_copy, a, u, 256, 512)
+            if i == 0:
+                cast(nc.vector.tensor_copy, a, u, 512, 768)
+                cast(nc.scalar.copy, a, u, 768, 896)
+                cast(nc.gpsimd.tensor_copy, a, u, 896, 1024)
+            else:
+                cast(nc.scalar.copy, a, u, 512, 768)
+                cast(nc.gpsimd.tensor_copy, a, u, 768, 1024)
+            if i == 1:
+                gather_plain(0, 0, 0)
+                gather_plain(0, 0, 1)
+                gather_plain(0, 1, 0)
+                weave_scalar(0, 0, 0, 256)
+                weave_gpsimd(0, 0, 256, 512)
+                gather_plain(0, 1, 1)
+            if i == 2:
+                gather_step(1, 0, 0)
+                weave_scalar(0, 1, 0, 256)
+                weave_gpsimd(0, 1, 256, 512)
+                gather_plain(1, 0, 1)
+        gather_step(1, 1, 0)
+        quantise(0, 0)
+        quantise(1, 0)
+        gather_plain(1, 1, 1)
+        weave_gpsimd(1, 1, 0, 512)
+        quantise(0, 1)
+
+        merged = [held.tile([P, T], F32, name=f"merged{t}") for t in range(NT)]
+
+        def multiply(acc, e, t, h, c0, n):
+            for a in range(PASSES):
+                nc.tensor.matmul_mx(
+                    out=acc,
+                    lhsT=words_of(e, a, t),
+                    lhsT_scale=w_sc[:, (e * PASSES + a) * N + P * t : (e * PASSES + a) * N + P * (t + 1)],
+                    rhs=codes[a][h][:, c0 : c0 + n].bitcast(FP8X4),
+                    rhs_scale=x_sc[a][h][:, c0 : c0 + n],
+                    start=(a == 0),
+                    stop=(a == PASSES - 1),
+                )
+
+        def piece(t, h, s0, n, mul_eng, add_eng):
+            y_bank = psum.tile([P, H], F32, name="bank")
+            for c in range(0, n, C):
+                multiply(y_bank[:, c : c + C], (H * h + s0 + c) // C, t, h, s0 + c, C)
+            if n == H:
+                s_bank = psum.tile([P, H], F32, name="bank")
+                s_acc = s_bank[:]
+                multiply(s_acc, E, t, h, s0, n)
+            else:
+                s_acc = y_bank[:, n : 2 * n]
+                for c in range(0, n, C):
+                    multiply(y_bank[:, n + c : n + c + C], E, t, h, s0 + c, C)
+            y = work.tile([P, H], F32, name="y")
+            for c in range(0, n, C):
+                e = (H * h + s0 + c) // C
+                nc.scalar.activation(y[:, c : c + C], y_bank[:, c : c + C], RELU, bias=bias[:, t, e : e + 1])
+            s = work.tile([P, H], F32, name="s")
+            nc.scalar.activation(s[:, 0:n], s_acc, RELU, bias=bias[:, t, E : E + 1])
+            gated = work.tile([P, H], F32, name="gated")
+            mul_eng.tensor_tensor(gated[:, 0:n], y[:, 0:n], gates[h][:, s0 : s0 + n], MULT)
+            z = work.tile([P, H], F32, name="z")
+            add_eng.tensor_tensor(z[:, 0:n], gated[:, 0:n], s[:, 0:n], ADD)
+            first = (H * h + s0) // 16
+            nc.vector.tensor_copy(merged[t][:].indirect(offsets[:, first : first + n // 16]), z[:, 0:n])
+
+        piece(0, 0, 0, 256, nc.vector, nc.vector)
+        quantise(1, 1)
+        piece(0, 0, 256, 256, nc.vector, nc.vector)
+        piece(1, 0, 0, H, nc.gpsimd, nc.gpsimd)
+        piece(2, 0, 0, H, nc.gpsimd, nc.gpsimd)
+        for t in range(NT):
+            piece(t, 1, 0, H, nc.gpsimd, nc.gpsimd)
+            nc.sync.dma_start(out=out[P * t : P * (t + 1), :], in_=merged[t][:])

@@ -37,26 +37,25 @@ def tile_moe_shr_lin_relu_kernel(tc, xT, w_words, w_scales, b, gate, offs, out):
         offsets = held.tile([P, E * C // 16], U16, name="offsets")
         nc.sync.dma_start(offsets[:], offs)
 
+        w_sc = held.tile([P, (E + 1) * PASSES * N], U8, name="w_sc", align_bytes=64)
+        nc.vector.memset(w_sc[:].bitcast(I32), 0)
+        scales_in = w_scales.bitcast(I32)
+        for q in range(4):
+            nc.gpsimd.dma_start(
+                out=w_sc[32 * q : 32 * q + 4, :].bitcast(I32).rearrange("q (g n) -> q g n", n=N // 4),
+                in_=scales_in[:, :, 4 * q : 4 * q + 4, :].rearrange("e a q n -> q (e a) n"),
+            )
         bias = held.tile([P, NT, E + 1], F32, name="bias")
-        nc.scalar.dma_start(out=bias[:], in_=b.rearrange("(t p) e -> p t e", p=P))
-
         raw = [[held.tile([P, 2, T], F32, name=f"raw{a}{u}") for u in range(2)] for a in range(PASSES)]
         pair = [[held.tile([P, 2 * T], BF16, name=f"pair{a}{u}", align_bytes=64) for u in range(2)] for a in range(PASSES)]
         for a in range(PASSES):
             rows = xT[512 * a : 512 * (a + 1), :].rearrange("(p j) w -> p j w", j=4)
             for u in range(2):
-                for c in range(2):
-                    cols = slice(512 * c, 512 * (c + 1))
+                parts = 2 if a == u else 1
+                for c in range(parts):
+                    cols = slice(T // parts * c, T // parts * (c + 1))
                     nc.sync.dma_start(out=raw[a][u][:, :, cols], in_=rows[:, 2 * u : 2 * u + 2, cols])
 
-        w_sc = held.tile([P, (E + 1) * PASSES * N], U8, name="w_sc", align_bytes=64)
-        nc.vector.memset(w_sc[:].bitcast(I32), 0)
-        scales_in = w_scales.bitcast(I32)
-        for q in range(4):
-            nc.sync.dma_start(
-                out=w_sc[32 * q : 32 * q + 4, :].bitcast(I32).rearrange("q (g n) -> q g n", n=N // 4),
-                in_=scales_in[:, :, 4 * q : 4 * q + 4, :].rearrange("e a q n -> q (e a) n"),
-            )
         w_tile = [held.tile([P, n, PASSES, 2 * N], U8, name=f"w_tile{i}", align_bytes=64) for i, (e, n) in enumerate(W_LOADS)]
         gates = [held.tile([P, H], F32, name=f"gates{h}") for h in range(2)]
         words_in = w_words.bitcast(I32)
@@ -73,6 +72,7 @@ def tile_moe_shr_lin_relu_kernel(tc, xT, w_words, w_scales, b, gate, offs, out):
 
         load_words(0)
         load_words(1)
+        nc.gpsimd.dma_start(out=bias[:], in_=b.rearrange("(t p) e -> p t e", p=P))
         load_gates(0)
         load_words(2)
         load_words(3)
@@ -100,8 +100,10 @@ def tile_moe_shr_lin_relu_kernel(tc, xT, w_words, w_scales, b, gate, offs, out):
         def gather_plain(a, u, h):
             nc.vector.tensor_copy(planes[a][h][:, u, :], window(a, u, h))
 
-        def gather_step(a, u, h):
-            nc.vector.tensor_copy(grouped[a][h][:].bitcast(U32).rearrange("p (s u) -> p s u", u=2)[:, :, u], window(a, u, h))
+        def gather_step(a, u, h, s0, n):
+            dst = grouped[a][h][:].bitcast(U32).rearrange("p (s u) -> p s u", u=2)[:, s0 : s0 + n, u]
+            first = (H * h + s0) // 16
+            nc.vector.tensor_copy(dst, pair[a][u][:].bitcast(U32).indirect(offsets[:, first : first + n // 16]))
 
         def weave_scalar(a, h, s0, s1):
             src = planes[a][h][:].rearrange("p u s -> p (u s)").bitcast(BF16).rearrange("p (u s j) -> p s u j", u=2, j=2)
@@ -113,38 +115,35 @@ def tile_moe_shr_lin_relu_kernel(tc, xT, w_words, w_scales, b, gate, offs, out):
                 planes[a][h][:, :, s0:s1].rearrange("p u s -> p s u"),
             )
 
-        def quantise(a, h):
-            nc.vector.quantize_mx(out=codes[a][h][:].bitcast(FP8X4), scales=x_sc[a][h][:], in_=grouped[a][h][:])
+        def quantise(a, h, s0, n):
+            nc.vector.quantize_mx(
+                out=codes[a][h][:, s0 : s0 + n].bitcast(FP8X4),
+                scales=x_sc[a][h][:, s0 : s0 + n],
+                in_=grouped[a][h][:, 4 * s0 : 4 * (s0 + n)],
+            )
 
         for i in range(4):
             a, u = divmod(i, 2)
             cast(nc.scalar.copy, a, u, 0, 256)
-            cast(nc.gpsimd.tensor_copy, a, u, 256, 512)
             if i == 0:
-                cast(nc.vector.tensor_copy, a, u, 512, 768)
-                cast(nc.scalar.copy, a, u, 768, 896)
-                cast(nc.gpsimd.tensor_copy, a, u, 896, 1024)
+                cast(nc.vector.tensor_copy, a, u, 256, 512)
+                cast(nc.scalar.copy, a, u, 512, 704)
+                cast(nc.vector.tensor_copy, a, u, 704, 1024)
             else:
+                cast(nc.gpsimd.tensor_copy, a, u, 256, 512)
                 cast(nc.scalar.copy, a, u, 512, 768)
                 cast(nc.gpsimd.tensor_copy, a, u, 768, 1024)
+            if i < 2:
+                gather_plain(a, u, 0)
+            elif i == 2:
+                gather_step(a, u, 0, 0, H)
+                quantise(0, 0, 0, H)
             if i == 1:
-                gather_plain(0, 0, 0)
-                gather_plain(0, 0, 1)
-                gather_plain(0, 1, 0)
                 weave_scalar(0, 0, 0, 256)
                 weave_gpsimd(0, 0, 256, 512)
-                gather_plain(0, 1, 1)
-            if i == 2:
-                gather_step(1, 0, 0)
-                weave_scalar(0, 1, 0, 256)
-                weave_gpsimd(0, 1, 256, 512)
-                gather_plain(1, 0, 1)
-        gather_step(1, 1, 0)
-        quantise(0, 0)
-        quantise(1, 0)
-        gather_plain(1, 1, 1)
-        weave_gpsimd(1, 1, 0, 512)
-        quantise(0, 1)
+        for s0 in (0, 256):
+            gather_step(1, 1, 0, s0, 256)
+            quantise(1, 0, s0, 256)
 
         merged = [held.tile([P, T], F32, name=f"merged{t}") for t in range(NT)]
 
@@ -161,23 +160,40 @@ def tile_moe_shr_lin_relu_kernel(tc, xT, w_words, w_scales, b, gate, offs, out):
                 )
 
         def piece(t, h, s0, n, mul_eng, add_eng):
-            y_bank = psum.tile([P, H], F32, name="bank")
-            for c in range(0, n, C):
-                multiply(y_bank[:, c : c + C], (H * h + s0 + c) // C, t, h, s0 + c, C)
+            cuts = [(c, min(C, n - c)) for c in range(0, n, C)]
             if n == H:
+                y_bank = psum.tile([P, H], F32, name="bank")
                 s_bank = psum.tile([P, H], F32, name="bank")
-                s_acc = s_bank[:]
-                multiply(s_acc, E, t, h, s0, n)
+                y_acc = [y_bank[:, c : c + C] for c, w in cuts]
+                s_acc = [s_bank[:, c : c + C] for c, w in cuts]
+                s_out = [(s_bank[:], 0, n)]
+            elif s0 == 0:
+                y_acc, s_acc = [], []
+                for c, w in cuts:
+                    bank_y = psum.tile([P, H], F32, name="bank")
+                    bank_s = psum.tile([P, H], F32, name="bank")
+                    y_acc.append(bank_y[:, 0:C])
+                    s_acc.append(bank_s[:, 0:C])
+                s_out = [(s_acc[i], c, C) for i, (c, w) in enumerate(cuts)]
             else:
-                s_acc = y_bank[:, n : 2 * n]
-                for c in range(0, n, C):
-                    multiply(y_bank[:, n + c : n + c + C], E, t, h, s0 + c, C)
+                bank = psum.tile([P, H], F32, name="bank")
+                y_acc = [bank[:, c : c + C] for c, w in cuts]
+                s_acc = [bank[:, n + c : n + c + C] for c, w in cuts]
+                s_out = [(bank[:, n : 2 * n], 0, n)]
+            for i, (c, w) in enumerate(cuts):
+                multiply(y_acc[i], (H * h + s0 + c) // C, t, h, s0 + c, C)
+            if n == H and h == 1:
+                multiply(s_bank[:], E, t, h, 0, H)
+            else:
+                for i, (c, w) in enumerate(cuts):
+                    multiply(s_acc[i], E, t, h, s0 + c, C)
             y = work.tile([P, H], F32, name="y")
             for c in range(0, n, C):
                 e = (H * h + s0 + c) // C
-                nc.scalar.activation(y[:, c : c + C], y_bank[:, c : c + C], RELU, bias=bias[:, t, e : e + 1])
+                nc.scalar.activation(y[:, c : c + C], y_acc[c // C], RELU, bias=bias[:, t, e : e + 1])
             s = work.tile([P, H], F32, name="s")
-            nc.scalar.activation(s[:, 0:n], s_acc, RELU, bias=bias[:, t, E : E + 1])
+            for acc, c, w in s_out:
+                nc.scalar.activation(s[:, c : c + w], acc, RELU, bias=bias[:, t, E : E + 1])
             gated = work.tile([P, H], F32, name="gated")
             mul_eng.tensor_tensor(gated[:, 0:n], y[:, 0:n], gates[h][:, s0 : s0 + n], MULT)
             z = work.tile([P, H], F32, name="z")
@@ -186,10 +202,15 @@ def tile_moe_shr_lin_relu_kernel(tc, xT, w_words, w_scales, b, gate, offs, out):
             nc.vector.tensor_copy(merged[t][:].indirect(offsets[:, first : first + n // 16]), z[:, 0:n])
 
         piece(0, 0, 0, 256, nc.vector, nc.vector)
-        quantise(1, 1)
         piece(0, 0, 256, 256, nc.vector, nc.vector)
         piece(1, 0, 0, H, nc.gpsimd, nc.gpsimd)
         piece(2, 0, 0, H, nc.gpsimd, nc.gpsimd)
+        for a in range(PASSES):
+            for u in range(2):
+                gather_plain(a, u, 1)
+            weave_scalar(a, 1, 0, 256)
+            weave_gpsimd(a, 1, 256, 512)
+            quantise(a, 1, 0, H)
         for t in range(NT):
             piece(t, 1, 0, H, nc.gpsimd, nc.gpsimd)
             nc.sync.dma_start(out=out[P * t : P * (t + 1), :], in_=merged[t][:])

from contextlib import ExitStack

import concourse.mybir as mybir

K, T, E, C, N = 1024, 1024, 8, 128, 384

F32 = mybir.dt.float32
BF16 = mybir.dt.bfloat16
I32 = mybir.dt.int32
U32 = mybir.dt.uint32
U16 = mybir.dt.uint16
U8 = mybir.dt.uint8
FP8X4 = mybir.dt.float8_e4m3fn_x4
FP4X4 = mybir.dt.float4_e2m1fn_x4
COPY = mybir.ActivationFunctionType.Copy
RELU = mybir.ActivationFunctionType.Relu
MULT = mybir.AluOpType.mult
ADD = mybir.AluOpType.add

P = 128
PASSES = K // 512
H = 512
NT = N // P
W_LOADS = ((E, 1), (0, 2), (2, 2), (4, 4))

FLOPS = 2 * K * N * T * 2
BYTES = K * T * 4 + (E + 1) * K * N // 2 + (E + 1) * (K // 32) * N + N * (E + 1) * 4 + E * C * 4 + E * C * 2 + N * T * 4


def tile_moe_shr_lin_relu_kernel(tc, xT, w_words, w_scales, b, gate, offs, out):
    nc = tc.nc
    with ExitStack() as ctx:
        held = ctx.enter_context(tc.tile_pool(name="held", bufs=1))
        work = ctx.enter_context(tc.tile_pool(name="work", bufs=3))
        psum = ctx.enter_context(tc.psum_pool(name="psum", bufs=8))

        offsets = held.tile([P, E * C // 16], U16, name="offsets")
        nc.sync.dma_start(offsets[:], offs)

        w_sc = held.tile([P, (E + 1) * PASSES * N], U8, name="w_sc", align_bytes=64)
        nc.vector.memset(w_sc[:].bitcast(I32), 0)
        scales_in = w_scales.bitcast(I32)
        for q in range(4):
            nc.gpsimd.dma_start(
                out=w_sc[32 * q : 32 * q + 4, :].bitcast(I32).rearrange("q (g n) -> q g n", n=N // 4),
                in_=scales_in[:, :, 4 * q : 4 * q + 4, :].rearrange("e a q n -> q (e a) n"),
            )
        bias = held.tile([P, NT, E + 1], F32, name="bias")
        raw = [[held.tile([P, 2, T], F32, name=f"raw{a}{u}") for u in range(2)] for a in range(PASSES)]
        pair = [[held.tile([P, 2 * T], BF16, name=f"pair{a}{u}", align_bytes=64) for u in range(2)] for a in range(PASSES)]
        for a in range(PASSES):
            rows = xT[512 * a : 512 * (a + 1), :].rearrange("(p j) w -> p j w", j=4)
            for u in range(2):
                parts = 2 if a == u else 1
                for c in range(parts):
                    cols = slice(T // parts * c, T // parts * (c + 1))
                    nc.sync.dma_start(out=raw[a][u][:, :, cols], in_=rows[:, 2 * u : 2 * u + 2, cols])

        w_tile = [held.tile([P, n, PASSES, 2 * N], U8, name=f"w_tile{i}", align_bytes=64) for i, (e, n) in enumerate(W_LOADS)]
        gates = [held.tile([P, H], F32, name=f"gates{h}") for h in range(2)]
        words_in = w_words.bitcast(I32)

        def load_words(i):
            e, n = W_LOADS[i]
            nc.sync.dma_start(
                out=w_tile[i][:].rearrange("p e a n -> p (e a n)").bitcast(I32).rearrange("p (g n) -> p g n", n=N // 2),
                in_=words_in[e : e + n].rearrange("e a p n -> p (e a) n"),
            )

        def load_gates(h):
            nc.sync.dma_start(out=gates[h][:], in_=gate[0:P, H * h : H * (h + 1)])

        load_words(0)
        load_words(1)
        nc.gpsimd.dma_start(out=bias[:], in_=b.rearrange("(t p) e -> p t e", p=P))
        load_gates(0)
        load_words(2)
        load_words(3)
        load_gates(1)

        def words_of(e, a, t):
            for i, (first, n) in enumerate(W_LOADS):
                if first <= e < first + n:
                    return w_tile[i][:, e - first, a, 2 * P * t : 2 * P * (t + 1)].bitcast(FP4X4)

        def cast(engine_call, a, u, c0, c1):
            engine_call(
                pair[a][u][:, 2 * c0 : 2 * c1].rearrange("p (w j) -> p w j", j=2),
                raw[a][u][:, :, c0:c1].rearrange("p j w -> p w j"),
            )

        planes = [[held.tile([P, 2, H], U32, name=f"planes{a}{h}", align_bytes=64) for h in range(2)] for a in range(PASSES)]
        grouped = [[held.tile([P, 4 * H], BF16, name=f"grouped{a}{h}", align_bytes=64) for h in range(2)] for a in range(PASSES)]
        codes = [[held.tile([P, H], U32, name=f"codes{a}{h}", align_bytes=64) for h in range(2)] for a in range(PASSES)]
        x_sc = [[held.tile([P, H], U8, name=f"x_sc{a}{h}", align_bytes=64) for h in range(2)] for a in range(PASSES)]

        def window(a, u, h):
            return pair[a][u][:].bitcast(U32).indirect(offsets[:, 32 * h : 32 * (h + 1)])

        def gather_plain(a, u, h):
            nc.vector.tensor_copy(planes[a][h][:, u, :], window(a, u, h))

        def gather_step(a, u, h, s0, n):
            dst = grouped[a][h][:].bitcast(U32).rearrange("p (s u) -> p s u", u=2)[:, s0 : s0 + n, u]
            first = (H * h + s0) // 16
            nc.vector.tensor_copy(dst, pair[a][u][:].bitcast(U32).indirect(offsets[:, first : first + n // 16]))

        def weave_scalar(a, h, s0, s1):
            src = planes[a][h][:].rearrange("p u s -> p (u s)").bitcast(BF16).rearrange("p (u s j) -> p s u j", u=2, j=2)
            nc.scalar.copy(grouped[a][h][:].rearrange("p (s u j) -> p s u j", u=2, j=2)[:, s0:s1], src[:, s0:s1])

        def weave_gpsimd(a, h, s0, s1):
            nc.gpsimd.tensor_copy(
                grouped[a][h][:].bitcast(U32).rearrange("p (s u) -> p s u", u=2)[:, s0:s1],
                planes[a][h][:, :, s0:s1].rearrange("p u s -> p s u"),
            )

        def quantise(a, h, s0, n):
            nc.vector.quantize_mx(
                out=codes[a][h][:, s0 : s0 + n].bitcast(FP8X4),
                scales=x_sc[a][h][:, s0 : s0 + n],
                in_=grouped[a][h][:, 4 * s0 : 4 * (s0 + n)],
            )

        for i in range(4):
            a, u = divmod(i, 2)
            cast(nc.scalar.copy, a, u, 0, 256)
            if i == 0:
                cast(nc.vector.tensor_copy, a, u, 256, 512)
                cast(nc.scalar.copy, a, u, 512, 704)
                cast(nc.vector.tensor_copy, a, u, 704, 1024)
            else:
                cast(nc.gpsimd.tensor_copy, a, u, 256, 512)
                cast(nc.scalar.copy, a, u, 512, 768)
                cast(nc.gpsimd.tensor_copy, a, u, 768, 1024)
            if i < 2:
                gather_plain(a, u, 0)
            elif i == 2:
                gather_step(a, u, 0, 0, H)
                quantise(0, 0, 0, H)
            if i == 1:
                weave_scalar(0, 0, 0, 256)
                weave_gpsimd(0, 0, 256, 512)
        for s0 in (0, 256):
            gather_step(1, 1, 0, s0, 256)
            quantise(1, 0, s0, 256)

        merged = [held.tile([P, T], F32, name=f"merged{t}") for t in range(NT)]

        def multiply(acc, e, t, h, c0, n):
            for a in range(PASSES):
                nc.tensor.matmul_mx(
                    out=acc,
                    lhsT=words_of(e, a, t),
                    lhsT_scale=w_sc[:, (e * PASSES + a) * N + P * t : (e * PASSES + a) * N + P * (t + 1)],
                    rhs=codes[a][h][:, c0 : c0 + n].bitcast(FP8X4),
                    rhs_scale=x_sc[a][h][:, c0 : c0 + n],
                    start=(a == 0),
                    stop=(a == PASSES - 1),
                )

        def piece(t, h, s0, n, mul_eng, add_eng):
            cuts = [(c, min(C, n - c)) for c in range(0, n, C)]
            if n == H:
                y_bank = psum.tile([P, H], F32, name="bank")
                s_bank = psum.tile([P, H], F32, name="bank")
                y_acc = [y_bank[:, c : c + C] for c, w in cuts]
                s_acc = [s_bank[:, c : c + C] for c, w in cuts]
                s_out = [(s_bank[:], 0, n)]
            elif s0 == 0:
                y_acc, s_acc = [], []
                for c, w in cuts:
                    bank_y = psum.tile([P, H], F32, name="bank")
                    bank_s = psum.tile([P, H], F32, name="bank")
                    y_acc.append(bank_y[:, 0:C])
                    s_acc.append(bank_s[:, 0:C])
                s_out = [(s_acc[i], c, C) for i, (c, w) in enumerate(cuts)]
            else:
                bank = psum.tile([P, H], F32, name="bank")
                y_acc = [bank[:, c : c + C] for c, w in cuts]
                s_acc = [bank[:, n + c : n + c + C] for c, w in cuts]
                s_out = [(bank[:, n : 2 * n], 0, n)]
            for i, (c, w) in enumerate(cuts):
                multiply(y_acc[i], (H * h + s0 + c) // C, t, h, s0 + c, C)
            if n == H and h == 1:
                multiply(s_bank[:], E, t, h, 0, H)
            else:
                for i, (c, w) in enumerate(cuts):
                    multiply(s_acc[i], E, t, h, s0 + c, C)
            y = work.tile([P, H], F32, name="y")
            for c in range(0, n, C):
                e = (H * h + s0 + c) // C
                nc.scalar.activation(y[:, c : c + C], y_acc[c // C], RELU, bias=bias[:, t, e : e + 1])
            s = work.tile([P, H], F32, name="s")
            for acc, c, w in s_out:
                nc.scalar.activation(s[:, c : c + w], acc, RELU, bias=bias[:, t, E : E + 1])
            gated = work.tile([P, H], F32, name="gated")
            mul_eng.tensor_tensor(gated[:, 0:n], y[:, 0:n], gates[h][:, s0 : s0 + n], MULT)
            z = work.tile([P, H], F32, name="z")
            add_eng.tensor_tensor(z[:, 0:n], gated[:, 0:n], s[:, 0:n], ADD)
            first = (H * h + s0) // 16
            nc.vector.tensor_copy(merged[t][:].indirect(offsets[:, first : first + n // 16]), z[:, 0:n])

        piece(0, 0, 0, 256, nc.vector, nc.vector)
        piece(0, 0, 256, 256, nc.vector, nc.vector)
        piece(1, 0, 0, H, nc.gpsimd, nc.gpsimd)
        piece(2, 0, 0, H, nc.gpsimd, nc.gpsimd)
        for a in range(PASSES):
            for u in range(2):
                gather_plain(a, u, 1)
            weave_scalar(a, 1, 0, 256)
            weave_gpsimd(a, 1, 256, 512)
            quantise(a, 1, 0, H)
        for t in range(NT):
            piece(t, 1, 0, H, nc.gpsimd, nc.gpsimd)
            nc.sync.dma_start(out=out[P * t : P * (t + 1), :], in_=merged[t][:])
